import numpy as np
import ml_dtypes


def mxq(x, axis, fmt="e4m3"):
    dtype, down = {"e4m3": (ml_dtypes.float8_e4m3fn, 7), "e5m2": (ml_dtypes.float8_e5m2, 14)}[fmt]
    v = np.moveaxis(np.asarray(x, np.float32).astype(ml_dtypes.bfloat16).astype(np.float64), axis, -1)
    blocks = v.reshape(v.shape[:-1] + (-1, 32))
    amax = np.abs(blocks).max(-1, keepdims=True)
    byte = np.maximum(np.where(amax > 0, np.frexp(amax)[1] - 1 + 127, 0) - down, 1)
    scale = np.exp2(byte - 127.0)
    codes = (blocks / scale).astype(np.float32).astype(dtype).astype(np.float64)
    return np.moveaxis((codes * scale).reshape(v.shape), -1, axis)


WIDE = False


def mx_kscale(k):
    if not WIDE:
        return np.ones(k)
    levels = np.array([30, -30])
    if k % 512:
        return np.exp2(np.random.permutation(np.resize(levels, k // 32))).repeat(32)
    a = np.empty((k // 512, 16))
    for p in range(k // 512):
        a[p, :8] = np.random.permutation(np.resize(levels, 8))
        for g in range(8):
            far = levels[np.abs(levels - a[p, g]) >= 10]
            a[p, g + 8] = far[np.random.randint(len(far))]
    return np.exp2(a.ravel()).repeat(32)


BF16 = ml_dtypes.bfloat16


def bf(x):
    return np.asarray(x, np.float32).astype(BF16)


def f64(x):
    return np.asarray(x).astype(np.float64)


E2M1 = np.array([0.0, 0.5, 1.0, 1.5, 2.0, 3.0, 4.0, 6.0, -0.0, -0.5, -1.0, -1.5, -2.0, -3.0, -4.0, -6.0])


def pack_weight(w, fmt):
    k, n = w.shape
    w = f64(bf(w)).reshape(k // 32, 32, n)
    amax = np.abs(w).max(1)
    if fmt in ("e4m3", "e5m2"):
        byte = np.frexp(amax)[1] - 1 + 127 - (7 if fmt == "e4m3" else 14)
    else:
        mant, ex = np.frexp(amax / 6.0)
        byte = np.where(mant > 0.5, ex, ex - 1) + 127
    byte = np.clip(np.where(amax > 0, byte, 1), 1, 254)
    scaled = (w * np.exp2(127.0 - byte)[:, None, :]).reshape(k, n).astype(np.float32)
    by_word = np.ascontiguousarray(scaled.reshape(k // 512, 128, 4, n).transpose(0, 1, 3, 2))
    if fmt in ("e4m3", "e5m2"):
        words = by_word.astype(ml_dtypes.float8_e4m3fn if fmt == "e4m3" else ml_dtypes.float8_e5m2).view(np.uint8)
    else:
        c = by_word.astype(ml_dtypes.float4_e2m1fn).view(np.uint8) & 0xF
        words = c[..., 0::2] | (c[..., 1::2] << 4)
    return np.ascontiguousarray(words), np.ascontiguousarray(byte.astype(np.uint8).reshape(k // 512, 16, n))


def unpack_weight(words, scales, fmt):
    g, p, n, _ = words.shape
    if fmt in ("e4m3", "e5m2"):
        vals = np.ascontiguousarray(words).view(ml_dtypes.float8_e4m3fn if fmt == "e4m3" else ml_dtypes.float8_e5m2).astype(np.float64)
    else:
        nib = np.empty((g, p, n, 4), np.uint8)
        nib[..., 0::2] = words & 0xF
        nib[..., 1::2] = words >> 4
        vals = E2M1[nib]
    vals = vals * np.repeat(np.exp2(scales.astype(np.float64) - 127.0), 8, axis=1)[..., None]
    return vals.transpose(0, 1, 3, 2).reshape(g * 512, n)


C, D, L, B = 1024, 2048, 512, 1024


def setup_inputs():
    s = mx_kscale(C)
    t = mx_kscale(D)
    G = 0.6 * np.random.standard_normal((C, B)) * np.exp(0.7 * np.random.standard_normal((C, B)))
    g_words, g_scales = pack_weight(G * s[:, None], "e5m2")
    return {"g_words": g_words, "g_scales": g_scales,
            "a": bf(np.random.standard_normal((C, D)) / np.sqrt(C) / s[:, None] * t),
            "cost": bf(0.5 * np.random.standard_normal(D) * t),
            "slope": bf(1.0 - np.tanh(np.random.standard_normal((D, B))) ** 2),
            "w": bf(np.random.standard_normal((D, L)) / np.sqrt(D) / t[:, None]),
            "tau": bf(0.3 + 0.1 * np.abs(np.random.standard_normal(L))),
            "z": bf(np.random.standard_normal((L, B)))}


def reference(g_words, g_scales, a, cost, slope, w, tau, z):
    G = unpack_weight(g_words, g_scales, "e5m2")
    ag = mxq(f64(a), 0, "e4m3").T @ G
    h = (ag + f64(cost)[:, None]) * f64(slope)
    wh = mxq(f64(w), 0, "e4m3").T @ mxq(h, 0, "e5m2")
    return wh + f64(tau)[:, None] * f64(z)

@@ -1,0 +1,264 @@
+from contextlib import ExitStack
+
+import concourse.mybir as mybir
+
+C, D, L, B = 1024, 2048, 512, 1024
+FLOPS = 2 * C * D * B + 2 * D * L * B
+
+F32 = mybir.dt.float32
+BF16 = mybir.dt.bfloat16
+I32 = mybir.dt.int32
+U32 = mybir.dt.uint32
+U8 = mybir.dt.uint8
+E4M3 = mybir.dt.float8_e4m3fn_x4
+E5M2 = mybir.dt.float8_e5m2_x4
+ADD = mybir.AluOpType.add
+MULT = mybir.AluOpType.mult
+
+P = 128
+N = 512
+GROUPS = C // 512
+CHUNKS = D // 512
+HALVES = B // N
+TILES = [(0, 0), (1, 0), (0, 1), (2, 0), (1, 1), (3, 0), (2, 1), (3, 1)]
+
+
+def tile_augmented_lagrangian_latent_gradient_e3_kernel(
+    tc, g_words, g_scales, a, cost, slope, w, tau, z, out
+):
+    nc = tc.nc
+    with ExitStack() as ctx:
+        keep = ctx.enter_context(tc.tile_pool(name="keep", bufs=1))
+        stage = ctx.enter_context(tc.tile_pool(name="stage", bufs=3))
+        psum = ctx.enter_context(tc.psum_pool(name="psum", bufs=1))
+        ctx.enter_context(tc.manual_schedule())
+
+        gs = keep.tile([P, GROUPS, B], U8, name="gs", align_bytes=64)
+        gq = [keep.tile([P, GROUPS, N], U32, name="gq%d" % h, align_bytes=64) for h in range(HALVES)]
+        a_raw = [[keep.tile([P, 4, 512], BF16, name="ar%d%d" % (c, g), align_bytes=64) for g in range(GROUPS)] for c in range(CHUNKS)]
+        aq = [[keep.tile([P, 512], U32, name="aq%d%d" % (c, g), align_bytes=64) for g in range(GROUPS)] for c in range(CHUNKS)]
+        asc = [[keep.tile([P, 512], U8, name="as%d%d" % (c, g), align_bytes=64) for g in range(GROUPS)] for c in range(CHUNKS)]
+        sl = [keep.tile([P, 4, B], BF16, name="sl%d" % c, align_bytes=64) for c in range(CHUNKS)]
+        w_raw = [keep.tile([P, 4, L], BF16, name="wr%d" % c, align_bytes=64) for c in range(CHUNKS)]
+        wq = [keep.tile([P, L], U32, name="wq%d" % c, align_bytes=64) for c in range(CHUNKS)]
+        wsc = [keep.tile([P, L], U8, name="ws%d" % c, align_bytes=64) for c in range(CHUNKS)]
+        hq = [[keep.tile([P, N], U32, name="hq%d%d" % (c, h), align_bytes=64) for h in range(HALVES)] for c in range(CHUNKS)]
+        hsc = [[keep.tile([P, N], U8, name="hs%d%d" % (c, h), align_bytes=64) for h in range(HALVES)] for c in range(CHUNKS)]
+        zt = keep.tile([P, 4, B], BF16, name="zt", align_bytes=64)
+        ct = keep.tile([P, CHUNKS, 4], BF16, name="ct", align_bytes=64)
+        tt = keep.tile([P, 4], BF16, name="tt", align_bytes=64)
+
+        nc.vector.memset(gs[:].rearrange("p g n -> p (g n)").bitcast(U32), 0)
+        scales_i = g_scales.bitcast(I32)
+        for q in range(4):
+            nc.scalar.dma_start(
+                out=gs[32 * q : 32 * q + 4, :, :].bitcast(I32),
+                in_=scales_i[:, 4 * q : 4 * q + 4, :].rearrange("g q n -> q g n"),
+            )
+        nc.scalar.dma_start(out=ct[:], in_=cost.rearrange("(c p t) -> p c t", c=CHUNKS, t=4))
+        nc.scalar.dma_start(out=tt[:], in_=tau.rearrange("(p m) -> p m", m=4))
+
+        def load_a(c, g):
+            nc.sync.dma_start(
+                out=a_raw[c][g][:],
+                in_=a[512 * g : 512 * g + 512, 512 * c : 512 * c + 512].rearrange("(p j) w -> p j w", j=4),
+            )
+
+        g_bytes = g_words.rearrange("g p n t -> p g (n t)")
+
+        def load_g(h):
+            nc.sync.dma_start(out=gq[h][:].bitcast(I32), in_=g_bytes[:, :, 4 * N * h : 4 * N * (h + 1)].bitcast(I32))
+
+        def load_slope(c, h):
+            lo, hi = N * h, N * (h + 1)
+            nc.sync.dma_start(
+                out=sl[c][:, :, lo:hi],
+                in_=slope[512 * c : 512 * c + 512, lo:hi].rearrange("(p t) b -> p t b", t=4),
+            )
+
+        def load_w(c):
+            nc.sync.dma_start(out=w_raw[c][:], in_=w[512 * c : 512 * c + 512, :].rearrange("(p j) l -> p j l", j=4))
+
+        load_a(0, 0)
+        load_a(0, 1)
+        load_a(1, 0)
+        load_a(1, 1)
+        load_g(0)
+        load_slope(0, 0)
+        load_a(2, 0)
+        load_a(2, 1)
+        load_slope(1, 0)
+        load_a(3, 0)
+        load_g(1)
+        load_slope(0, 1)
+        load_a(3, 1)
+        load_slope(2, 0)
+        load_w(0)
+        load_slope(1, 1)
+        load_w(1)
+        load_slope(3, 0)
+        load_w(2)
+        load_slope(2, 1)
+        load_w(3)
+        load_slope(3, 1)
+        nc.sync.dma_start(out=zt[:], in_=z.rearrange("(p m) b -> p m b", m=4))
+
+        def copy_on(eng, dst, src):
+            if eng == "v":
+                nc.vector.tensor_copy(out=dst, in_=src)
+            else:
+                nc.scalar.copy(dst, src)
+
+        def il_cols(dst, src, shares):
+            d = dst[:].rearrange("p (t c i j) -> p t c j i", t=4, i=2, j=4)
+            s = src.rearrange("p j (c i t) -> p t c j i", i=2, t=4)
+            for eng, lo, hi in shares:
+                copy_on(eng, d[:, :, lo:hi], s[:, :, lo:hi])
+
+        grouped = {}
+
+        def il_a(c, g, shares):
+            ag = stage.tile([P, 2048], BF16, name="ag", align_bytes=64)
+            grouped["a", c, g] = ag
+            il_cols(ag, a_raw[c][g][:], shares)
+
+        def q_a(c, g):
+            nc.vector.quantize_mx(out=aq[c][g][:].bitcast(E4M3), scales=asc[c][g][:], in_=grouped["a", c, g][:])
+
+        def il_w(c, shares):
+            wg = stage.tile([P, 2048], BF16, name="wg", align_bytes=64)
+            grouped["w", c] = wg
+            il_cols(wg, w_raw[c][:], shares)
+
+        def q_w(c):
+            nc.vector.quantize_mx(out=wq[c][:].bitcast(E4M3), scales=wsc[c][:], in_=grouped["w", c][:])
+
+        banks = {}
+
+        def stage1(i, t, gs_range=range(GROUPS)):
+            c, h = TILES[i]
+            if 0 in gs_range:
+                banks[i, t] = psum.tile([P, N], F32, name="s%d" % t)
+            for g in gs_range:
+                nc.tensor.matmul_mx(
+                    out=banks[i, t][:],
+                    lhsT=aq[c][g][:, 128 * t : 128 * t + 128].bitcast(E4M3),
+                    lhsT_scale=asc[c][g][:, 128 * t : 128 * t + 128],
+                    rhs=gq[h][:, g, :].bitcast(E5M2),
+                    rhs_scale=gs[:, g, N * h : N * (h + 1)],
+                    start=(g == 0),
+                    stop=(g == GROUPS - 1),
+                )
+
+        def new_h(i):
+            hr = stage.tile([P, 4, N], BF16, name="hr", align_bytes=64)
+            grouped["r", i] = hr
+
+        def stt(i, t):
+            c, h = TILES[i]
+            nc.vector.scalar_tensor_tensor(
+                out=grouped["r", i][:, t, :],
+                in0=banks[i, t][:],
+                scalar=ct[:, c, t : t + 1],
+                in1=sl[c][:, t, N * h : N * (h + 1)],
+                op0=ADD,
+                op1=MULT,
+            )
+
+        def il_h(i, shares):
+            hg = stage.tile([P, 2048], BF16, name="hg", align_bytes=64)
+            grouped["h", i] = hg
+            d = hg[:].rearrange("p (c i t) -> p c t i", i=4, t=4)
+            s = grouped["r", i][:].rearrange("p t (c i) -> p c t i", i=4)
+            for eng, lo, hi in shares:
+                copy_on(eng, d[:, lo:hi], s[:, lo:hi])
+
+        def q_h(i):
+            c, h = TILES[i]
+            nc.vector.quantize_mx(out=hq[c][h][:].bitcast(E5M2), scales=hsc[c][h][:], in_=grouped["h", i][:])
+
+        acc = {}
+
+        def stage2(c, h, m):
+            nc.tensor.matmul_mx(
+                out=acc[h, m][:],
+                lhsT=wq[c][:, 128 * m : 128 * m + 128].bitcast(E4M3),
+                lhsT_scale=wsc[c][:, 128 * m : 128 * m + 128],
+                rhs=hq[c][h][:].bitcast(E5M2),
+                rhs_scale=hsc[c][h][:],
+                start=(c == 0),
+                stop=(c == CHUNKS - 1),
+            )
+
+        out_rows = out.rearrange("(p m) b -> p m b", m=4)
+
+        def finish(h, m):
+            o = keep.tile([P, N], F32, name="o%d%d" % (h, m), align_bytes=64)
+            nc.vector.scalar_tensor_tensor(
+                out=o[:],
+                in0=zt[:, m, N * h : N * (h + 1)],
+                scalar=tt[:, m : m + 1],
+                in1=acc[h, m][:],
+                op0=MULT,
+                op1=ADD,
+            )
+            nc.sync.dma_start(out=out_rows[:, m, N * h : N * (h + 1)], in_=o[:])
+
+        def shares(v, n):
+            cuts = [("v", 0, v), ("s", v, n)]
+            return [x for x in cuts if x[1] < x[2]]
+
+        half = shares(32, 64)
+        quarter = shares(16, 64)
+        il_a(0, 0, half)
+        il_a(0, 1, half)
+        q_a(0, 0)
+        il_a(1, 0, half)
+        q_a(0, 1)
+        il_a(1, 1, half)
+        q_a(1, 0)
+        q_a(1, 1)
+        for g in range(GROUPS):
+            for t in range(4):
+                stage1(0, t, [g])
+        for m in range(4):
+            acc[0, m] = psum.tile([P, N], F32, name="acc%d" % m)
+        last = len(TILES) - 1
+        extra = [[("a", 2, 0), ("a", 2, 1)], [("a", 3, 0)], [("a", 3, 1)], [("w", 0)], [("w", 1)], [("w", 2)], [("w", 3)], []]
+        for i in range(last + 1):
+            new_h(i)
+            for t in range(4):
+                stt(i, t)
+                if i < last:
+                    stage1(i + 1, t)
+            for x in extra[i]:
+                if x[0] == "a":
+                    il_a(x[1], x[2], half if x[1] == 2 else quarter)
+                else:
+                    il_w(x[1], quarter)
+            if i < last:
+                il_h(i, shares(0, 128))
+            for x in extra[i - 1] if i > 0 else []:
+                if x[0] == "a":
+                    q_a(x[1], x[2])
+                else:
+                    q_w(x[1])
+            if i > 0:
+                q_h(i - 1)
+            k = i - 4
+            if k >= 0:
+                for m in range(4):
+                    stage2(k, 0, m)
+        for m in range(4):
+            acc[1, m] = psum.tile([P, N], F32, name="s%d" % m)
+            for k in range(CHUNKS - 1):
+                stage2(k, 1, m)
+        il_h(last, shares(64, 128))
+        finish(0, 0)
+        q_h(last)
+        for m in range(4):
+            stage2(CHUNKS - 1, 1, m)
+        for m in range(1, 4):
+            finish(0, m)
+        for m in range(4):
+            finish(1, m)

@@ -110,10 +110,10 @@ def tile_augmented_lagrangian_latent_gradient_e3_kernel(
                 nc.scalar.copy(dst, src)
 
         def il_cols(dst, src, shares):
-            d = dst[:].rearrange("p (t c i j) -> p t c j i", t=4, i=2, j=4)
-            s = src.rearrange("p j (c i t) -> p t c j i", i=2, t=4)
+            d = dst[:].rearrange("p (t m j) -> p m j t", t=4, j=4)
+            s = src.rearrange("p j (m t) -> p m j t", t=4)
             for eng, lo, hi in shares:
-                copy_on(eng, d[:, :, lo:hi], s[:, :, lo:hi])
+                copy_on(eng, d[:, lo:hi], s[:, lo:hi])
 
         grouped = {}
 
@@ -208,8 +208,8 @@ def tile_augmented_lagrangian_latent_gradient_e3_kernel(
             cuts = [("v", 0, v), ("s", v, n)]
             return [x for x in cuts if x[1] < x[2]]
 
-        half = shares(32, 64)
-        quarter = shares(16, 64)
+        half = shares(64, 128)
+        quarter = shares(32, 128)
         il_a(0, 0, half)
         il_a(0, 1, half)
         q_a(0, 0)

@@ -16,11 +16,17 @@ ADD = mybir.AluOpType.add
 MULT = mybir.AluOpType.mult
 
 P = 128
+PACK = 4
+K = P * PACK
 N = 512
-GROUPS = C // 512
-CHUNKS = D // 512
+GROUPS = C // K
+CHUNKS = D // K
 HALVES = B // N
-TILES = [(0, 0), (1, 0), (0, 1), (2, 0), (1, 1), (3, 0), (2, 1), (3, 1)]
+
+TILES = [(0, 0), (1, 0), (0, 1), (1, 1), (2, 0), (3, 0), (2, 1), (3, 1)]
+
+HEAD = [("w", 0), ("a", 0, 0), ("a", 1, 0), ("w", 1), ("a", 0, 1), ("a", 1, 1), ("a", 2, 0)]
+BESIDE = {0: [("a", 3, 0)], 2: [("a", 2, 1)], 3: [("a", 3, 1)], 4: [("w", 2)], 5: [("w", 3)]}
 
 
 def tile_augmented_lagrangian_latent_gradient_e3_kernel(
@@ -33,232 +39,210 @@ def tile_augmented_lagrangian_latent_gradient_e3_kernel(
         psum = ctx.enter_context(tc.psum_pool(name="psum", bufs=1))
         ctx.enter_context(tc.manual_schedule())
 
-        gs = keep.tile([P, GROUPS, B], U8, name="gs", align_bytes=64)
-        gq = [keep.tile([P, GROUPS, N], U32, name="gq%d" % h, align_bytes=64) for h in range(HALVES)]
-        a_raw = [[keep.tile([P, 4, 512], BF16, name="ar%d%d" % (c, g), align_bytes=64) for g in range(GROUPS)] for c in range(CHUNKS)]
-        aq = [[keep.tile([P, 512], U32, name="aq%d%d" % (c, g), align_bytes=64) for g in range(GROUPS)] for c in range(CHUNKS)]
-        asc = [[keep.tile([P, 512], U8, name="as%d%d" % (c, g), align_bytes=64) for g in range(GROUPS)] for c in range(CHUNKS)]
-        sl = [keep.tile([P, 4, B], BF16, name="sl%d" % c, align_bytes=64) for c in range(CHUNKS)]
-        w_raw = [keep.tile([P, 4, L], BF16, name="wr%d" % c, align_bytes=64) for c in range(CHUNKS)]
-        wq = [keep.tile([P, L], U32, name="wq%d" % c, align_bytes=64) for c in range(CHUNKS)]
-        wsc = [keep.tile([P, L], U8, name="ws%d" % c, align_bytes=64) for c in range(CHUNKS)]
-        hq = [[keep.tile([P, N], U32, name="hq%d%d" % (c, h), align_bytes=64) for h in range(HALVES)] for c in range(CHUNKS)]
-        hsc = [[keep.tile([P, N], U8, name="hs%d%d" % (c, h), align_bytes=64) for h in range(HALVES)] for c in range(CHUNKS)]
-        zt = keep.tile([P, 4, B], BF16, name="zt", align_bytes=64)
-        ct = keep.tile([P, CHUNKS, 4], BF16, name="ct", align_bytes=64)
-        tt = keep.tile([P, 4], BF16, name="tt", align_bytes=64)
+        def sbuf(name, shape, dtype):
+            return keep.tile(shape, dtype, name=name, align_bytes=64)
 
-        nc.vector.memset(gs[:].rearrange("p g n -> p (g n)").bitcast(U32), 0)
-        scales_i = g_scales.bitcast(I32)
-        for q in range(4):
-            nc.scalar.dma_start(
-                out=gs[32 * q : 32 * q + 4, :, :].bitcast(I32),
-                in_=scales_i[:, 4 * q : 4 * q + 4, :].rearrange("g q n -> q g n"),
-            )
-        nc.scalar.dma_start(out=ct[:], in_=cost.rearrange("(c p t) -> p c t", c=CHUNKS, t=4))
-        nc.scalar.dma_start(out=tt[:], in_=tau.rearrange("(p m) -> p m", m=4))
+        g_codes = [sbuf("g_codes%d" % h, [P, GROUPS, N], U32) for h in range(HALVES)]
+        g_planes = sbuf("g_planes", [P, GROUPS, B], U8)
+        a_raw = [[sbuf("a_raw%d%d" % (q, g), [P, PACK, D // 2], BF16) for g in range(GROUPS)] for q in range(2)]
+        a_codes = [[sbuf("a_codes%d%d" % (c, g), [P, K], U32) for g in range(GROUPS)] for c in range(CHUNKS)]
+        a_planes = [[sbuf("a_planes%d%d" % (c, g), [P, K], U8) for g in range(GROUPS)] for c in range(CHUNKS)]
+        slopes = [sbuf("slopes%d" % c, [P, PACK, B], BF16) for c in range(CHUNKS)]
+        w_raw = [sbuf("w_raw%d" % c, [P, PACK, L], BF16) for c in range(CHUNKS)]
+        w_codes = [sbuf("w_codes%d" % c, [P, L], U32) for c in range(CHUNKS)]
+        w_planes = [sbuf("w_planes%d" % c, [P, L], U8) for c in range(CHUNKS)]
+        h_codes = {tile: sbuf("h_codes%d%d" % tile, [P, N], U32) for tile in TILES}
+        h_planes = {tile: sbuf("h_planes%d%d" % tile, [P, N], U8) for tile in TILES}
+        costs = sbuf("costs", [P, CHUNKS, PACK], BF16)
+        taus = sbuf("taus", [P, PACK], BF16)
+        z_rows = sbuf("z_rows", [P, PACK, B], BF16)
 
-        def load_a(c, g):
-            nc.sync.dma_start(
-                out=a_raw[c][g][:],
-                in_=a[512 * g : 512 * g + 512, 512 * c : 512 * c + 512].rearrange("(p j) w -> p j w", j=4),
-            )
-
-        g_bytes = g_words.rearrange("g p n t -> p g (n t)")
+        def load_a(q, g):
+            source = a[K * g : K * (g + 1), q * (D // 2) : (q + 1) * (D // 2)]
+            nc.sync.dma_start(out=a_raw[q][g][:], in_=source.rearrange("(p j) d -> p j d", j=PACK))
 
         def load_g(h):
-            nc.sync.dma_start(out=gq[h][:].bitcast(I32), in_=g_bytes[:, :, 4 * N * h : 4 * N * (h + 1)].bitcast(I32))
+            source = g_words.rearrange("g p n t -> p g (n t)")[:, :, PACK * N * h : PACK * N * (h + 1)]
+            nc.sync.dma_start(out=g_codes[h][:].bitcast(I32), in_=source.bitcast(I32))
 
-        def load_slope(c, h):
-            lo, hi = N * h, N * (h + 1)
-            nc.sync.dma_start(
-                out=sl[c][:, :, lo:hi],
-                in_=slope[512 * c : 512 * c + 512, lo:hi].rearrange("(p t) b -> p t b", t=4),
-            )
+        def load_g_planes():
+            source = g_scales.bitcast(I32)
+            for q in range(4):
+                nc.sync.dma_start(
+                    out=g_planes[32 * q : 32 * q + 4, :, :].bitcast(I32),
+                    in_=source[:, 4 * q : 4 * q + 4, :].rearrange("g r n -> r g n"),
+                )
+
+        def load_slope(c, columns):
+            source = slope[K * c : K * (c + 1), columns]
+            nc.sync.dma_start(out=slopes[c][:, :, columns], in_=source.rearrange("(p t) n -> p t n", t=PACK))
 
         def load_w(c):
-            nc.sync.dma_start(out=w_raw[c][:], in_=w[512 * c : 512 * c + 512, :].rearrange("(p j) l -> p j l", j=4))
+            nc.sync.dma_start(out=w_raw[c][:], in_=w[K * c : K * (c + 1), :].rearrange("(p j) l -> p j l", j=PACK))
 
-        load_a(0, 0)
-        load_a(0, 1)
-        load_a(1, 0)
-        load_a(1, 1)
-        load_g(0)
-        load_slope(0, 0)
-        load_a(2, 0)
-        load_a(2, 1)
-        load_slope(1, 0)
-        load_a(3, 0)
-        load_g(1)
-        load_slope(0, 1)
-        load_a(3, 1)
-        load_slope(2, 0)
+        nc.vector.memset(g_planes[:].rearrange("p g n -> p (g n)").bitcast(U32), 0)
+
+        first_half, second_half, whole = slice(0, N), slice(N, B), slice(0, B)
         load_w(0)
-        load_slope(1, 1)
+        load_a(0, 0)
         load_w(1)
-        load_slope(3, 0)
+        load_a(0, 1)
+        load_g(0)
+        load_a(1, 0)
+        load_g_planes()
+        nc.sync.dma_start(out=costs[:], in_=cost.rearrange("(c p t) -> p c t", c=CHUNKS, t=PACK))
+        load_slope(0, first_half)
+        load_slope(1, whole)
+        load_g(1)
+        load_slope(0, second_half)
+        load_a(1, 1)
+        load_slope(2, whole)
+        nc.sync.dma_start(out=taus[:], in_=tau.rearrange("(p m) -> p m", m=PACK))
         load_w(2)
-        load_slope(2, 1)
+        load_slope(3, whole)
         load_w(3)
-        load_slope(3, 1)
-        nc.sync.dma_start(out=zt[:], in_=z.rearrange("(p m) b -> p m b", m=4))
-
-        def copy_on(eng, dst, src):
-            if eng == "v":
-                nc.vector.tensor_copy(out=dst, in_=src)
-            else:
-                nc.scalar.copy(dst, src)
-
-        def il_cols(dst, src, shares):
-            d = dst[:].rearrange("p (t m j) -> p m j t", t=4, j=4)
-            s = src.rearrange("p j (m t) -> p m j t", t=4)
-            for eng, lo, hi in shares:
-                copy_on(eng, d[:, lo:hi], s[:, lo:hi])
+        nc.sync.dma_start(out=z_rows[:], in_=z.rearrange("(p m) n -> p m n", m=PACK))
 
         grouped = {}
 
-        def il_a(c, g, shares):
-            ag = stage.tile([P, 2048], BF16, name="ag", align_bytes=64)
-            grouped["a", c, g] = ag
-            il_cols(ag, a_raw[c][g][:], shares)
+        def interleave(x):
+            if x[0] == "a":
+                c, g = x[1], x[2]
+                source = a_raw[c // 2][g][:, :, K * (c % 2) : K * (c % 2 + 1)]
+            else:
+                source = w_raw[x[1]][:]
+            grouped[x] = stage.tile([P, K * PACK], BF16, name="grouped", align_bytes=64, bufs=5)
+            dst = grouped[x][:].rearrange("p (t m i j) -> p t m j i", t=PACK, i=2, j=PACK)
+            src = source.rearrange("p j (m i t) -> p t m j i", i=2, t=PACK)
+            pairs = K // PACK // 2
+            cut = 0 if x[:2] == ("a", CHUNKS - 1) else pairs // 2
+            if cut:
+                nc.vector.tensor_copy(out=dst[:, :, :cut], in_=src[:, :, :cut])
+            nc.scalar.copy(dst[:, :, cut:], src[:, :, cut:])
 
-        def q_a(c, g):
-            nc.vector.quantize_mx(out=aq[c][g][:].bitcast(E4M3), scales=asc[c][g][:], in_=grouped["a", c, g][:])
-
-        def il_w(c, shares):
-            wg = stage.tile([P, 2048], BF16, name="wg", align_bytes=64)
-            grouped["w", c] = wg
-            il_cols(wg, w_raw[c][:], shares)
-
-        def q_w(c):
-            nc.vector.quantize_mx(out=wq[c][:].bitcast(E4M3), scales=wsc[c][:], in_=grouped["w", c][:])
+        def quantise(x):
+            if x[0] == "a":
+                codes, planes = a_codes[x[1]][x[2]], a_planes[x[1]][x[2]]
+            else:
+                codes, planes = w_codes[x[1]], w_planes[x[1]]
+            nc.vector.quantize_mx(out=codes[:].bitcast(E4M3), scales=planes[:], in_=grouped[x][:])
 
         banks = {}
 
-        def stage1(i, t, gs_range=range(GROUPS)):
+        def first_product(i, t, groups):
             c, h = TILES[i]
-            if 0 in gs_range:
-                banks[i, t] = psum.tile([P, N], F32, name="s%d" % t)
-            for g in gs_range:
+            columns = slice(P * t, P * (t + 1))
+            for g in groups:
+                if g == 0:
+                    banks[i, t] = psum.tile([P, N], F32, name="bank%d" % t)
                 nc.tensor.matmul_mx(
                     out=banks[i, t][:],
-                    lhsT=aq[c][g][:, 128 * t : 128 * t + 128].bitcast(E4M3),
-                    lhsT_scale=asc[c][g][:, 128 * t : 128 * t + 128],
-                    rhs=gq[h][:, g, :].bitcast(E5M2),
-                    rhs_scale=gs[:, g, N * h : N * (h + 1)],
+                    lhsT=a_codes[c][g][:, columns].bitcast(E4M3),
+                    lhsT_scale=a_planes[c][g][:, columns],
+                    rhs=g_codes[h][:, g, :].bitcast(E5M2),
+                    rhs_scale=g_planes[:, g, N * h : N * (h + 1)],
                     start=(g == 0),
                     stop=(g == GROUPS - 1),
                 )
 
-        def new_h(i):
-            hr = stage.tile([P, 4, N], BF16, name="hr", align_bytes=64)
-            grouped["r", i] = hr
+        h_rows, h_grouped = {}, {}
 
-        def stt(i, t):
+        def read_banks(i):
             c, h = TILES[i]
-            nc.vector.scalar_tensor_tensor(
-                out=grouped["r", i][:, t, :],
-                in0=banks[i, t][:],
-                scalar=ct[:, c, t : t + 1],
-                in1=sl[c][:, t, N * h : N * (h + 1)],
-                op0=ADD,
-                op1=MULT,
+            h_rows[i] = stage.tile([P, PACK, N], BF16, name="h_rows", align_bytes=64)
+            for t in range(PACK):
+                nc.vector.scalar_tensor_tensor(
+                    out=h_rows[i][:, t, :],
+                    in0=banks[i, t][:],
+                    scalar=costs[:, c, t : t + 1],
+                    in1=slopes[c][:, t, N * h : N * (h + 1)],
+                    op0=ADD,
+                    op1=MULT,
+                )
+
+        def interleave_h(i):
+            h_grouped[i] = stage.tile([P, N * PACK], BF16, name="h_grouped", align_bytes=64)
+            nc.scalar.copy(
+                h_grouped[i][:].rearrange("p (n i t) -> p n t i", i=4, t=PACK),
+                h_rows[i][:].rearrange("p t (n i) -> p n t i", i=4),
             )
 
-        def il_h(i, shares):
-            hg = stage.tile([P, 2048], BF16, name="hg", align_bytes=64)
-            grouped["h", i] = hg
-            d = hg[:].rearrange("p (c i t) -> p c t i", i=4, t=4)
-            s = grouped["r", i][:].rearrange("p t (c i) -> p c t i", i=4)
-            for eng, lo, hi in shares:
-                copy_on(eng, d[:, lo:hi], s[:, lo:hi])
+        def quantise_h(i):
+            tile = TILES[i]
+            nc.vector.quantize_mx(out=h_codes[tile][:].bitcast(E5M2), scales=h_planes[tile][:], in_=h_grouped[i][:])
 
-        def q_h(i):
-            c, h = TILES[i]
-            nc.vector.quantize_mx(out=hq[c][h][:].bitcast(E5M2), scales=hsc[c][h][:], in_=grouped["h", i][:])
+        sums = {}
 
-        acc = {}
-
-        def stage2(c, h, m):
+        def second_product(c, h, m):
+            columns = slice(P * m, P * (m + 1))
             nc.tensor.matmul_mx(
-                out=acc[h, m][:],
-                lhsT=wq[c][:, 128 * m : 128 * m + 128].bitcast(E4M3),
-                lhsT_scale=wsc[c][:, 128 * m : 128 * m + 128],
-                rhs=hq[c][h][:].bitcast(E5M2),
-                rhs_scale=hsc[c][h][:],
+                out=sums[h, m][:],
+                lhsT=w_codes[c][:, columns].bitcast(E4M3),
+                lhsT_scale=w_planes[c][:, columns],
+                rhs=h_codes[c, h][:].bitcast(E5M2),
+                rhs_scale=h_planes[c, h][:],
                 start=(c == 0),
                 stop=(c == CHUNKS - 1),
             )
 
-        out_rows = out.rearrange("(p m) b -> p m b", m=4)
+        out_rows = out.rearrange("(p m) n -> p m n", m=PACK)
 
         def finish(h, m):
-            o = keep.tile([P, N], F32, name="o%d%d" % (h, m), align_bytes=64)
+            columns = slice(N * h, N * (h + 1))
+            result = stage.tile([P, N], F32, name="result", align_bytes=64, bufs=8)
             nc.vector.scalar_tensor_tensor(
-                out=o[:],
-                in0=zt[:, m, N * h : N * (h + 1)],
-                scalar=tt[:, m : m + 1],
-                in1=acc[h, m][:],
+                out=result[:],
+                in0=z_rows[:, m, columns],
+                scalar=taus[:, m : m + 1],
+                in1=sums[h, m][:],
                 op0=MULT,
                 op1=ADD,
             )
-            nc.sync.dma_start(out=out_rows[:, m, N * h : N * (h + 1)], in_=o[:])
+            nc.sync.dma_start(out=out_rows[:, m, columns], in_=result[:])
 
-        def shares(v, n):
-            cuts = [("v", 0, v), ("s", v, n)]
-            return [x for x in cuts if x[1] < x[2]]
-
-        half = shares(64, 128)
-        quarter = shares(32, 128)
-        il_a(0, 0, half)
-        il_a(0, 1, half)
-        q_a(0, 0)
-        il_a(1, 0, half)
-        q_a(0, 1)
-        il_a(1, 1, half)
-        q_a(1, 0)
-        q_a(1, 1)
+        for x, before in zip(HEAD, [None] + HEAD):
+            interleave(x)
+            if before:
+                quantise(before)
+        quantise(HEAD[-1])
         for g in range(GROUPS):
-            for t in range(4):
-                stage1(0, t, [g])
-        for m in range(4):
-            acc[0, m] = psum.tile([P, N], F32, name="acc%d" % m)
+            for t in range(PACK):
+                first_product(0, t, [g])
+        for m in range(PACK):
+            sums[0, m] = psum.tile([P, N], F32, name="sum%d" % m)
+
         last = len(TILES) - 1
-        extra = [[("a", 2, 0), ("a", 2, 1)], [("a", 3, 0)], [("a", 3, 1)], [("w", 0)], [("w", 1)], [("w", 2)], [("w", 3)], []]
+        ready = set(HEAD)
+        summed = 0
         for i in range(last + 1):
-            new_h(i)
-            for t in range(4):
-                stt(i, t)
-                if i < last:
-                    stage1(i + 1, t)
-            for x in extra[i]:
-                if x[0] == "a":
-                    il_a(x[1], x[2], half if x[1] == 2 else quarter)
-                else:
-                    il_w(x[1], quarter)
+            read_banks(i)
+            for x in BESIDE.get(i, []):
+                interleave(x)
             if i < last:
-                il_h(i, shares(0, 128))
-            for x in extra[i - 1] if i > 0 else []:
-                if x[0] == "a":
-                    q_a(x[1], x[2])
-                else:
-                    q_w(x[1])
+                interleave_h(i)
+            for x in BESIDE.get(i - 1, []):
+                quantise(x)
+                ready.add(x)
+            if i < last:
+                for t in range(PACK):
+                    first_product(i + 1, t, range(GROUPS))
             if i > 0:
-                q_h(i - 1)
-            k = i - 4
-            if k >= 0:
-                for m in range(4):
-                    stage2(k, 0, m)
-        for m in range(4):
-            acc[1, m] = psum.tile([P, N], F32, name="s%d" % m)
-            for k in range(CHUNKS - 1):
-                stage2(k, 1, m)
-        il_h(last, shares(64, 128))
-        finish(0, 0)
-        q_h(last)
-        for m in range(4):
-            stage2(CHUNKS - 1, 1, m)
-        for m in range(1, 4):
+                quantise_h(i - 1)
+                ready.add(TILES[i - 1])
+            while summed < CHUNKS and ("w", summed) in ready and (summed, 0) in ready:
+                for m in range(PACK):
+                    second_product(summed, 0, m)
+                summed += 1
+
+        for m in range(PACK):
             finish(0, m)
-        for m in range(4):
+        interleave_h(last)
+        for m in range(PACK):
+            sums[1, m] = psum.tile([P, N], F32, name="bank%d" % m)
+        for c in range(CHUNKS):
+            if c == CHUNKS - 1:
+                quantise_h(last)
+            for m in range(PACK):
+                second_product(c, 1, m)
+        for m in range(PACK):
             finish(1, m)

from contextlib import ExitStack

import concourse.mybir as mybir

C, D, L, B = 1024, 2048, 512, 1024
FLOPS = 2 * C * D * B + 2 * D * L * B

F32 = mybir.dt.float32
BF16 = mybir.dt.bfloat16
I32 = mybir.dt.int32
U32 = mybir.dt.uint32
U8 = mybir.dt.uint8
E4M3 = mybir.dt.float8_e4m3fn_x4
E5M2 = mybir.dt.float8_e5m2_x4
ADD = mybir.AluOpType.add
MULT = mybir.AluOpType.mult

P = 128
PACK = 4
K = P * PACK
N = 512
GROUPS = C // K
CHUNKS = D // K
HALVES = B // N

TILES = [(0, 0), (1, 0), (0, 1), (1, 1), (2, 0), (3, 0), (2, 1), (3, 1)]

HEAD = [("w", 0), ("a", 0, 0), ("a", 1, 0), ("w", 1), ("a", 0, 1), ("a", 1, 1), ("a", 2, 0)]
BESIDE = {0: [("a", 3, 0)], 2: [("a", 2, 1)], 3: [("a", 3, 1)], 4: [("w", 2)], 5: [("w", 3)]}


def tile_augmented_lagrangian_latent_gradient_e3_kernel(
    tc, g_words, g_scales, a, cost, slope, w, tau, z, out
):
    nc = tc.nc
    with ExitStack() as ctx:
        keep = ctx.enter_context(tc.tile_pool(name="keep", bufs=1))
        stage = ctx.enter_context(tc.tile_pool(name="stage", bufs=3))
        psum = ctx.enter_context(tc.psum_pool(name="psum", bufs=1))
        ctx.enter_context(tc.manual_schedule())

        def sbuf(name, shape, dtype):
            return keep.tile(shape, dtype, name=name, align_bytes=64)

        g_codes = [sbuf("g_codes%d" % h, [P, GROUPS, N], U32) for h in range(HALVES)]
        g_planes = sbuf("g_planes", [P, GROUPS, B], U8)
        a_raw = [[sbuf("a_raw%d%d" % (q, g), [P, PACK, D // 2], BF16) for g in range(GROUPS)] for q in range(2)]
        a_codes = [[sbuf("a_codes%d%d" % (c, g), [P, K], U32) for g in range(GROUPS)] for c in range(CHUNKS)]
        a_planes = [[sbuf("a_planes%d%d" % (c, g), [P, K], U8) for g in range(GROUPS)] for c in range(CHUNKS)]
        slopes = [sbuf("slopes%d" % c, [P, PACK, B], BF16) for c in range(CHUNKS)]
        w_raw = [sbuf("w_raw%d" % c, [P, PACK, L], BF16) for c in range(CHUNKS)]
        w_codes = [sbuf("w_codes%d" % c, [P, L], U32) for c in range(CHUNKS)]
        w_planes = [sbuf("w_planes%d" % c, [P, L], U8) for c in range(CHUNKS)]
        h_codes = {tile: sbuf("h_codes%d%d" % tile, [P, N], U32) for tile in TILES}
        h_planes = {tile: sbuf("h_planes%d%d" % tile, [P, N], U8) for tile in TILES}
        costs = sbuf("costs", [P, CHUNKS, PACK], BF16)
        taus = sbuf("taus", [P, PACK], BF16)
        z_rows = sbuf("z_rows", [P, PACK, B], BF16)

        def load_a(q, g):
            source = a[K * g : K * (g + 1), q * (D // 2) : (q + 1) * (D // 2)]
            nc.sync.dma_start(out=a_raw[q][g][:], in_=source.rearrange("(p j) d -> p j d", j=PACK))

        def load_g(h):
            source = g_words.rearrange("g p n t -> p g (n t)")[:, :, PACK * N * h : PACK * N * (h + 1)]
            nc.sync.dma_start(out=g_codes[h][:].bitcast(I32), in_=source.bitcast(I32))

        def load_g_planes():
            source = g_scales.bitcast(I32)
            for q in range(4):
                nc.sync.dma_start(
                    out=g_planes[32 * q : 32 * q + 4, :, :].bitcast(I32),
                    in_=source[:, 4 * q : 4 * q + 4, :].rearrange("g r n -> r g n"),
                )

        def load_slope(c, columns):
            source = slope[K * c : K * (c + 1), columns]
            nc.sync.dma_start(out=slopes[c][:, :, columns], in_=source.rearrange("(p t) n -> p t n", t=PACK))

        def load_w(c):
            nc.sync.dma_start(out=w_raw[c][:], in_=w[K * c : K * (c + 1), :].rearrange("(p j) l -> p j l", j=PACK))

        nc.vector.memset(g_planes[:].rearrange("p g n -> p (g n)").bitcast(U32), 0)

        first_half, second_half, whole = slice(0, N), slice(N, B), slice(0, B)
        load_w(0)
        load_a(0, 0)
        load_w(1)
        load_a(0, 1)
        load_g(0)
        load_a(1, 0)
        load_g_planes()
        nc.sync.dma_start(out=costs[:], in_=cost.rearrange("(c p t) -> p c t", c=CHUNKS, t=PACK))
        load_slope(0, first_half)
        load_slope(1, whole)
        load_g(1)
        load_slope(0, second_half)
        load_a(1, 1)
        load_slope(2, whole)
        nc.sync.dma_start(out=taus[:], in_=tau.rearrange("(p m) -> p m", m=PACK))
        load_w(2)
        load_slope(3, whole)
        load_w(3)
        nc.sync.dma_start(out=z_rows[:], in_=z.rearrange("(p m) n -> p m n", m=PACK))

        grouped = {}

        def interleave(x):
            if x[0] == "a":
                c, g = x[1], x[2]
                source = a_raw[c // 2][g][:, :, K * (c % 2) : K * (c % 2 + 1)]
            else:
                source = w_raw[x[1]][:]
            grouped[x] = stage.tile([P, K * PACK], BF16, name="grouped", align_bytes=64, bufs=5)
            dst = grouped[x][:].rearrange("p (t m i j) -> p t m j i", t=PACK, i=2, j=PACK)
            src = source.rearrange("p j (m i t) -> p t m j i", i=2, t=PACK)
            pairs = K // PACK // 2
            cut = 0 if x[:2] == ("a", CHUNKS - 1) else pairs // 2
            if cut:
                nc.vector.tensor_copy(out=dst[:, :, :cut], in_=src[:, :, :cut])
            nc.scalar.copy(dst[:, :, cut:], src[:, :, cut:])

        def quantise(x):
            if x[0] == "a":
                codes, planes = a_codes[x[1]][x[2]], a_planes[x[1]][x[2]]
            else:
                codes, planes = w_codes[x[1]], w_planes[x[1]]
            nc.vector.quantize_mx(out=codes[:].bitcast(E4M3), scales=planes[:], in_=grouped[x][:])

        banks = {}

        def first_product(i, t, groups):
            c, h = TILES[i]
            columns = slice(P * t, P * (t + 1))
            for g in groups:
                if g == 0:
                    banks[i, t] = psum.tile([P, N], F32, name="bank%d" % t)
                nc.tensor.matmul_mx(
                    out=banks[i, t][:],
                    lhsT=a_codes[c][g][:, columns].bitcast(E4M3),
                    lhsT_scale=a_planes[c][g][:, columns],
                    rhs=g_codes[h][:, g, :].bitcast(E5M2),
                    rhs_scale=g_planes[:, g, N * h : N * (h + 1)],
                    start=(g == 0),
                    stop=(g == GROUPS - 1),
                )

        h_rows, h_grouped = {}, {}

        def read_banks(i):
            c, h = TILES[i]
            h_rows[i] = stage.tile([P, PACK, N], BF16, name="h_rows", align_bytes=64)
            for t in range(PACK):
                nc.vector.scalar_tensor_tensor(
                    out=h_rows[i][:, t, :],
                    in0=banks[i, t][:],
                    scalar=costs[:, c, t : t + 1],
                    in1=slopes[c][:, t, N * h : N * (h + 1)],
                    op0=ADD,
                    op1=MULT,
                )

        def interleave_h(i):
            h_grouped[i] = stage.tile([P, N * PACK], BF16, name="h_grouped", align_bytes=64)
            nc.scalar.copy(
                h_grouped[i][:].rearrange("p (n i t) -> p n t i", i=4, t=PACK),
                h_rows[i][:].rearrange("p t (n i) -> p n t i", i=4),
            )

        def quantise_h(i):
            tile = TILES[i]
            nc.vector.quantize_mx(out=h_codes[tile][:].bitcast(E5M2), scales=h_planes[tile][:], in_=h_grouped[i][:])

        sums = {}

        def second_product(c, h, m):
            columns = slice(P * m, P * (m + 1))
            nc.tensor.matmul_mx(
                out=sums[h, m][:],
                lhsT=w_codes[c][:, columns].bitcast(E4M3),
                lhsT_scale=w_planes[c][:, columns],
                rhs=h_codes[c, h][:].bitcast(E5M2),
                rhs_scale=h_planes[c, h][:],
                start=(c == 0),
                stop=(c == CHUNKS - 1),
            )

        out_rows = out.rearrange("(p m) n -> p m n", m=PACK)

        def finish(h, m):
            columns = slice(N * h, N * (h + 1))
            result = stage.tile([P, N], F32, name="result", align_bytes=64, bufs=8)
            nc.vector.scalar_tensor_tensor(
                out=result[:],
                in0=z_rows[:, m, columns],
                scalar=taus[:, m : m + 1],
                in1=sums[h, m][:],
                op0=MULT,
                op1=ADD,
            )
            nc.sync.dma_start(out=out_rows[:, m, columns], in_=result[:])

        for x, before in zip(HEAD, [None] + HEAD):
            interleave(x)
            if before:
                quantise(before)
        quantise(HEAD[-1])
        for g in range(GROUPS):
            for t in range(PACK):
                first_product(0, t, [g])
        for m in range(PACK):
            sums[0, m] = psum.tile([P, N], F32, name="sum%d" % m)

        last = len(TILES) - 1
        ready = set(HEAD)
        summed = 0
        for i in range(last + 1):
            read_banks(i)
            for x in BESIDE.get(i, []):
                interleave(x)
            if i < last:
                interleave_h(i)
            for x in BESIDE.get(i - 1, []):
                quantise(x)
                ready.add(x)
            if i < last:
                for t in range(PACK):
                    first_product(i + 1, t, range(GROUPS))
            if i > 0:
                quantise_h(i - 1)
                ready.add(TILES[i - 1])
            while summed < CHUNKS and ("w", summed) in ready and (summed, 0) in ready:
                for m in range(PACK):
                    second_product(summed, 0, m)
                summed += 1

        for m in range(PACK):
            finish(0, m)
        interleave_h(last)
        for m in range(PACK):
            sums[1, m] = psum.tile([P, N], F32, name="bank%d" % m)
        for c in range(CHUNKS):
            if c == CHUNKS - 1:
                quantise_h(last)
            for m in range(PACK):
                second_product(c, 1, m)
        for m in range(PACK):
            finish(1, m)
